import numpy as np, ml_dtypes
CORES = [7,15,23,39,47,63,71,79,87,95,119,127]
N = 12
DEG, TK = 5, 128
MASK = [[0,2,4,10,11],[1,2,3,6,9],[2,3,4,5,10],[2,3,7,8,9],[1,3,4,5,10],[3,4,5,7,8],[2,6,8,9,11],[4,5,6,7,9],[2,4,8,10,11],[2,4,7,8,9],[2,4,5,6,10],[0,3,8,10,11]]
def setup_inputs(rng):
    return {"x": rng.standard_normal((N, 128, TK), dtype=np.float32).astype(ml_dtypes.bfloat16), "w": rng.standard_normal((N, 128, DEG * 128), dtype=np.float32).astype(ml_dtypes.bfloat16)}
def setup_inputs_big(rng):
    d = setup_inputs(rng)
    for k in ("x", "w"): d[k] = (d[k].astype(np.float32) * 1024.0).astype(d[k].dtype)
    return d
def setup_inputs_small(rng):
    d = setup_inputs(rng)
    for k in ("x", "w"): d[k] = (d[k].astype(np.float32) * (1 / 1024.0)).astype(d[k].dtype)
    return d
def setup_inputs_apart(rng):
    d = setup_inputs(rng)
    f = (10.0 ** rng.permutation(np.linspace(-1.5, 1.5, N))).astype(np.float32).reshape(N, 1, 1)
    for k in ("x", "w"): d[k] = (d[k].astype(np.float32) * f).astype(d[k].dtype)
    return d
def reference(x, w):
    X, W = x.astype(np.float64), w.astype(np.float64)
    y = np.zeros((N, 128, TK))
    for r in range(N):
        for i, j in enumerate(MASK[r]):
            y[r] += W[r][:, 128 * i:128 * i + 128].T @ X[j]
    return {"y": y.astype(ml_dtypes.bfloat16 if x.dtype != np.float64 else np.float64)}

from concourse.bass import DstId, RemoteDMATransfer

N = 12
TK = 128
DEG = 5

SCRATCH = {
    "xd": ("dram", [128, TK], "bfloat16"),
    "xs": ("sbuf", [128, TK], "bfloat16"),
    "ws": ("sbuf", [128, DEG * 128], "bfloat16"),
    "land": ("sbuf", [128, N * TK], "bfloat16"),
    "acc": ("psum", [128, TK], "float32"),
    "ys": ("sbuf", [128, TK], "bfloat16"),
}
SEMAPHORES = ["xdl", "xsl", "wl", "sent", "mm", "cp", "st"] + ["a%d" % j for j in range(N)]

_CACHE = {}


def _timetable(mask):
    if "tt" in _CACHE:
        return _CACHE["tt"]
    out = {j: [r for r in range(N) if j in mask[r] and r != j] for j in range(N)}
    owners = sorted(out, key=lambda j: (-len(out[j]), j))
    used = [set() for _ in range(N)]
    res = {}

    def place(k):
        if k == len(owners):
            return True
        j = owners[k]
        seq = [None] * len(out[j])

        def fill(s, left):
            if s == len(seq):
                res[j] = list(seq)
                return place(k + 1)
            for r in left:
                if s not in used[r]:
                    used[r].add(s)
                    seq[s] = r
                    if fill(s + 1, [q for q in left if q != r]):
                        return True
                    used[r].discard(s)
            return False

        return fill(0, out[j])

    if not place(0):
        res = out
    _CACHE["tt"] = res
    return res


def rank_program(g, core, T, topo):
    rank = T.rank_of(core)
    if rank is None:
        return
    mask_tab = T.tables["MASK"]
    order = _timetable(mask_tab)
    cores = T.cores

    g.sync.dma_start(T.xd[:], T.x[:]).then_inc(T.sem.xdl, 16)
    g.sync.dma_start(T.xs[:], T.x[:]).then_inc(T.sem.xsl, 16)
    g.sync.dma_start(T.ws[:], T.w[:]).then_inc(T.sem.wl, 16)

    dests = order[rank]
    if dests:
        engines = topo.mask(core, cores[dests[0]])
        for r in dests:
            engines &= topo.mask(core, cores[r])
        n_eng = bin(engines).count("1")
        ids = []
        for r in dests:
            rid, pid, _se = topo.addr(cores[r])
            ids.append(DstId(rid=rid, pnc=pid))
        block = T.land[:, rank * TK:(rank + 1) * TK]
        g.wait_ge(T.sem.xdl, 16)
        g.remote_dma_fused(
            [RemoteDMATransfer(dst_ids=ids, dma_engine_mask=engines, remote_sem=T.sem["a%d" % rank],
                               srcs=[T.xd[:]], dsts=[block for _ in dests])],
            local_sem=T.sem.sent)

    row = mask_tab[rank]
    due = sorted((order[j].index(rank), j) for j in row if j != rank)
    seq = [rank] + [j for _s, j in due]
    g.tensor.wait_ge(T.sem.wl, 16)
    g.tensor.wait_ge(T.sem.xsl, 16)
    last = None
    for k, j in enumerate(seq):
        i = row.index(j)
        if j == rank:
            rhs = T.xs[:]
        else:
            src_eng = bin(_mask_of(topo, cores, order, j)).count("1")
            g.tensor.wait_ge(T.sem["a%d" % j], src_eng)
            rhs = T.land[:, j * TK:(j + 1) * TK]
        last = g.tensor.matmul(T.acc[:], T.ws[:, i * 128:(i + 1) * 128], rhs, k == 0, k == len(seq) - 1)
    last.then_inc(T.sem.mm, 1)

    g.vector.wait_ge(T.sem.mm, 1)
    g.vector.tensor_copy(T.ys[:], T.acc[:]).then_inc(T.sem.cp, 1)

    g.sync.wait_ge(T.sem.cp, 1)
    g.sync.dma_start(T.y[:], T.ys[:]).then_inc(T.sem.st, 16)
    g.sync.wait_ge(T.sem.st, 16)
    if dests:
        g.wait_ge(T.sem.sent, n_eng)


def _mask_of(topo, cores, order, j):
    m = topo.mask(cores[j], cores[order[j][0]])
    for r in order[j]:
        m &= topo.mask(cores[j], cores[r])
    return m
